import numpy as np
import ml_dtypes


def mxq(x, axis, fmt="e4m3"):
    dtype, down = {"e4m3": (ml_dtypes.float8_e4m3fn, 7), "e5m2": (ml_dtypes.float8_e5m2, 14)}[fmt]
    v = np.moveaxis(np.asarray(x, np.float32).astype(ml_dtypes.bfloat16).astype(np.float64), axis, -1)
    blocks = v.reshape(v.shape[:-1] + (-1, 32))
    amax = np.abs(blocks).max(-1, keepdims=True)
    byte = np.maximum(np.where(amax > 0, np.frexp(amax)[1] - 1 + 127, 0) - down, 1)
    scale = np.exp2(byte - 127.0)
    codes = (blocks / scale).astype(np.float32).astype(dtype).astype(np.float64)
    return np.moveaxis((codes * scale).reshape(v.shape), -1, axis)


WIDE = False


def mx_kscale(k):
    if not WIDE:
        return np.ones(k)
    levels = np.array([10, -10, 5, -5, 0])
    if k % 512:
        return np.exp2(np.random.permutation(np.resize(levels, k // 32))).repeat(32)
    a = np.empty((k // 512, 16))
    for p in range(k // 512):
        a[p, :8] = np.random.permutation(np.resize(levels, 8))
        for g in range(8):
            far = levels[np.abs(levels - a[p, g]) >= 10]
            a[p, g + 8] = far[np.random.randint(len(far))]
    return np.exp2(a.ravel()).repeat(32)


def f64(x):
    return np.asarray(x).astype(np.float64)


def striped(idx):
    return np.tile(np.asarray(idx).reshape(-1, 16).T, (8, 1)).astype(np.uint16)


def unstriped(offs):
    return offs[:16].T.reshape(-1).astype(np.int64)


def sigmoid(v):
    return 1.0 / (1.0 + np.exp(-v))


def bf(x):
    return np.asarray(x, np.float32).astype(ml_dtypes.bfloat16)


def planes(Y):
    r, m = Y.shape
    b = f64(bf(Y)).reshape(r // 32, 32, m)
    amax = np.abs(b).max(1)
    byte = np.clip(np.where(amax > 0, np.frexp(amax)[1] - 1 + 127 - 7, 1), 1, 254)
    codes = (b * np.exp2(127.0 - byte)[:, None, :]).reshape(r, m).astype(np.float32).astype(ml_dtypes.float8_e4m3fn).view(np.uint8)
    words = codes.reshape(r // 512, 128, 4, m).transpose(0, 1, 3, 2)
    return np.ascontiguousarray(words), np.ascontiguousarray(byte.astype(np.uint8).reshape(r // 512, 16, m))


D, T, I, Q = 512, 1024, 512, 512


def setup_inputs():
    n = np.random.standard_normal
    idx = np.random.permutation(T)[:I]
    idx2 = np.random.permutation(T)[:I]
    fd = mx_kscale(D)
    return {
        "query": (n((D, Q)) * 0.8 / np.sqrt(D) * fd[:, None]).astype(np.float32),
        "keys": (n((D, T)) + 0.7 * n((D, 1))).astype(np.float32),
        "steep": (np.random.uniform(4.0, 12.0, (I, 1))).astype(np.float32),
        "th": (np.random.uniform(0.3, 0.7, (I, 1))).astype(np.float32),
        "dsc": (np.random.uniform(0.5, 2.0, (1, D)) / fd).astype(np.float32),
        "offs": striped(idx),
        "offs2": striped(idx2),
    }


def reference(query, keys, steep, th, dsc, offs, offs2):
    idx = unstriped(offs)
    idx2 = unstriped(offs2)
    ka = f64(keys)[:, idx].T
    kb = f64(keys)[:, idx2].T
    al = sigmoid((np.mean(ka * kb, axis=1, keepdims=True) - f64(th)) * f64(steep)) * 0.5
    kj = (ka + (kb - ka) * al) * f64(dsc)
    km = kj.T
    queryq = mxq(f64(query), 0, "e4m3")
    kmq = mxq(km, 0, "e4m3")
    a = queryq.T @ kmq
    p = np.exp(a - np.max(a, axis=1, keepdims=True))
    y = p / np.sum(p, axis=1, keepdims=True) * 512.0
    words, scales = planes(y)
    return y, words, scales

@@ -1,0 +1,227 @@
+from contextlib import ExitStack
+
+import concourse.mybir as mybir
+from concourse.masks import make_identity
+
+F32 = mybir.dt.float32
+BF16 = mybir.dt.bfloat16
+U32 = mybir.dt.uint32
+I32 = mybir.dt.int32
+U16 = mybir.dt.uint16
+U8 = mybir.dt.uint8
+FP8X4 = mybir.dt.float8_e4m3fn_x4
+ALU = mybir.AluOpType
+ACT = mybir.ActivationFunctionType
+AXIS_X = mybir.AxisListType.X
+
+P = 128
+PACK = 4
+D, T, I, Q = 512, 1024, 512, 512
+CHUNK = 128
+CHUNKS = I // CHUNK
+HALF = I // 2
+PER_COLUMN = 16
+
+FLOPS = 2 * D * I * Q
+
+
+def tile_attend_similarmerge_pl_kernel(tc, query, keys, steep, th, dsc, offs, offs2, out_0, out_1, out_2):
+    nc = tc.nc
+    with ExitStack() as ctx:
+        keep = ctx.enter_context(tc.tile_pool(name="keep", bufs=1))
+        psum = ctx.enter_context(tc.psum_pool(name="psum", bufs=1))
+
+        offs_a = keep.tile([P, I // PER_COLUMN], U16, name="offs_a")
+        offs_b = keep.tile([P, I // PER_COLUMN], U16, name="offs_b")
+        planes = [keep.tile([P, T], F32, name="plane%d" % t) for t in range(PACK)]
+        q_raw = keep.tile([P, PACK, Q], F32, name="q_raw")
+        dsc_t = keep.tile([P, PACK], F32, name="dsc_t")
+        th_t = keep.tile([P, CHUNKS], F32, name="th_t")
+        steep_t = keep.tile([P, CHUNKS], F32, name="steep_t")
+
+        keys_v = keys.rearrange("(p t) n -> p t n", t=PACK)
+        nc.sync.dma_start(out=planes[0][:], in_=keys_v[:, 0, :])
+        nc.sync.dma_start(offs_a[:], offs)
+        nc.sync.dma_start(offs_b[:], offs2)
+        nc.sync.dma_start(out=dsc_t[:], in_=dsc.rearrange("o (p t) -> p (o t)", t=PACK))
+        nc.sync.dma_start(out=planes[1][:], in_=keys_v[:, 1, :])
+        nc.sync.dma_start(out=q_raw[:], in_=query.rearrange("(p t) n -> p t n", t=PACK))
+        nc.sync.dma_start(out=planes[2][:], in_=keys_v[:, 2, :])
+        nc.sync.dma_start(out=planes[3][:], in_=keys_v[:, 3, :])
+        with nc.allow_non_contiguous_dma(reason="one value a slot, slots on the partitions"):
+            nc.sync.dma_start(out=th_t[:], in_=th.rearrange("(c p) o -> p (c o)", p=P))
+            nc.sync.dma_start(out=steep_t[:], in_=steep.rearrange("(c p) o -> p (c o)", p=P))
+
+        ident = keep.tile([P, P], F32, name="ident")
+        make_identity(nc, ident[:])
+
+        warm = keep.tile([P, 1], F32, name="warm")
+        nc.scalar.activation(out=warm[:], in_=ident[:, 0:1], func=ACT.Exp)
+
+        neg_dsc = keep.tile([P, PACK], F32, name="neg_dsc")
+        nc.scalar.activation(out=neg_dsc[:], in_=dsc_t[:], func=ACT.Copy, scale=-1.0)
+
+        neg_ka = keep.tile([P, PACK, I], F32, name="neg_ka")
+        diff_banks = [psum.tile([P, PACK * P], F32, name="diff%d" % c) for c in range(CHUNKS)]
+        dot_banks = [psum.tile([P, PACK * P], F32, name="dot%d" % c) for c in range(CHUNKS)]
+        planes_done = [0] * CHUNKS
+
+        def gather(t, first, count, tag, last=False):
+            cols = slice(first // PER_COLUMN, (first + count) // PER_COLUMN)
+            ka = keep.tile([P, count], F32, name="ka", tag="ka" + tag)
+            kb = keep.tile([P, count], F32, name="kb", tag="kb" + tag)
+            prod = keep.tile([P, count], F32, name="prod%d_%d" % (t, first))
+            kb_s = keep.tile([P, count], F32, name="kb_s%d_%d" % (t, first))
+            nc.vector.tensor_copy(ka[:], planes[t][:].indirect(offs_a[:, cols]))
+            nc.vector.tensor_copy(kb[:], planes[t][:].indirect(offs_b[:, cols]))
+            nc.scalar.activation(out=neg_ka[:, t, first:first + count], in_=ka[:], func=ACT.Copy, scale=neg_dsc[:, t:t + 1])
+            if last:
+                nc.vector.tensor_tensor(prod[:], ka[:], kb[:], ALU.mult)
+                nc.scalar.activation(out=kb_s[:], in_=kb[:], func=ACT.Copy, scale=dsc_t[:, t:t + 1])
+            else:
+                nc.gpsimd.tensor_tensor(prod[:], ka[:], kb[:], ALU.mult)
+                nc.gpsimd.tensor_scalar(kb_s[:], kb[:], dsc_t[:, t:t + 1], 0.0, ALU.mult, ALU.add)
+            for c in range(first // CHUNK, (first + count) // CHUNK):
+                here = slice(c * CHUNK - first, (c + 1) * CHUNK - first)
+                nc.tensor.matmul(dot_banks[c][:, 0:P], prod[:, here], ident[:], is_transpose=True,
+                                 start=planes_done[c] == 0, stop=planes_done[c] == PACK - 1)
+                target = diff_banks[c][:, t * P:(t + 1) * P]
+                nc.tensor.matmul(target, neg_ka[:, t, c * CHUNK:(c + 1) * CHUNK], ident[:], is_transpose=True, start=True, stop=False)
+                nc.tensor.matmul(target, kb_s[:, here], ident[:], is_transpose=True, start=False, stop=True)
+                planes_done[c] = planes_done[c] + 1
+
+        tanh_scale = keep.tile([P, CHUNKS], F32, name="tanh_scale")
+        tanh_bias = keep.tile([P, CHUNKS], F32, name="tanh_bias")
+        dot = keep.tile([P, CHUNKS], F32, name="dot")
+        tanh_t = keep.tile([P, CHUNKS], F32, name="tanh_t")
+        share = keep.tile([P, CHUNKS], F32, name="share")
+        k_codes = keep.tile([P, I], U32, name="k_codes", align_bytes=64)
+        k_scales = keep.tile([P, I], U8, name="k_scales", align_bytes=64)
+        q_codes = keep.tile([P, Q], U32, name="q_codes", align_bytes=64)
+        q_scales = keep.tile([P, Q], U8, name="q_scales", align_bytes=64)
+
+        def quantise_query():
+            q_bf = keep.tile([P, PACK, P, PACK], BF16, name="q_bf", align_bytes=64)
+            for s0 in range(0, P, 32):
+                nc.scalar.copy(
+                    out=q_bf[:, :, s0:s0 + 32, :].rearrange("p r s t -> p s t r"),
+                    in_=q_raw[:, :, PACK * s0:PACK * (s0 + 32)].rearrange("p t (s r) -> p s t r", r=PACK),
+                )
+            nc.vector.quantize_mx(out=q_codes[:].bitcast(FP8X4), scales=q_scales[:], in_=q_bf[:].rearrange("p r s t -> p (r s t)"))
+
+        def merge(c):
+            col = slice(c, c + 1)
+            spent = keep.tile([P, P], F32, name="spent%d" % c)
+            nc.scalar.activation(out=spent[:], in_=dot_banks[c][:, 0:P], func=ACT.Copy, accum_out=dot[:, col])
+            nc.scalar.activation(out=tanh_t[:, col], in_=dot[:, col], func=ACT.Tanh, scale=tanh_scale[:, col], bias=tanh_bias[:, col])
+            nc.scalar.activation(out=share[:, col], in_=tanh_t[:, col], func=ACT.Copy, scale=0.25, bias=0.25)
+            step = keep.tile([P, PACK * P], F32, name="step%d" % c)
+            nc.scalar.activation(out=step[:], in_=diff_banks[c][:], func=ACT.Copy, scale=share[:, col])
+            for t in range(PACK):
+                nc.tensor.transpose(dot_banks[c][:, t * P:(t + 1) * P], step[:, t * P:(t + 1) * P], ident[:])
+            km = keep.tile([P, CHUNK, PACK], BF16, name="km%d" % c, align_bytes=64)
+            nc.vector.tensor_tensor(
+                km[:].rearrange("p (a i) t -> p a t i", i=PACK),
+                dot_banks[c][:].rearrange("p (t a i) -> p a t i", t=PACK, i=PACK),
+                neg_ka[:, :, c * CHUNK:(c + 1) * CHUNK].rearrange("p t (a i) -> p a t i", i=PACK),
+                ALU.subtract,
+            )
+            slots = slice(c * CHUNK, (c + 1) * CHUNK)
+            nc.vector.quantize_mx(out=k_codes[:, slots].bitcast(FP8X4), scales=k_scales[:, slots], in_=km[:].rearrange("p n t -> p (n t)"))
+
+        def score_view(h, r):
+            return diff_banks[2 * h + r // 2][:, (r % 2) * HALF:(r % 2 + 1) * HALF]
+
+        def scores(c):
+            slots = slice(c * CHUNK, (c + 1) * CHUNK)
+            for r in range(PACK):
+                rows = slice(r * P, (r + 1) * P)
+                nc.tensor.matmul_mx(
+                    out=score_view(c // 2, r)[:, (c % 2) * CHUNK:(c % 2 + 1) * CHUNK],
+                    lhsT=q_codes[:, rows].bitcast(FP8X4), lhsT_scale=q_scales[:, rows],
+                    rhs=k_codes[:, slots].bitcast(FP8X4), rhs_scale=k_scales[:, slots],
+                    start=True, stop=True,
+                )
+
+        gather(0, 0, I, "0")
+        gather(1, 0, I, "1")
+        quantise_query()
+        gather(2, 0, HALF, "2")
+        nc.gpsimd.tensor_scalar(tanh_scale[:], steep_t[:], 0.5 / D, 0.0, ALU.mult, ALU.add)
+        nc.gpsimd.tensor_tensor(tanh_bias[:], th_t[:], steep_t[:], ALU.mult)
+        nc.gpsimd.tensor_scalar(tanh_bias[:], tanh_bias[:], -0.5, 0.0, ALU.mult, ALU.add)
+        gather(3, 0, CHUNK, "early0")
+        gather(3, CHUNK, CHUNK, "early1")
+        gather(3, HALF, HALF, "3")
+        gather(2, 2 * CHUNK, CHUNK, "early0", last=True)
+        gather(2, 3 * CHUNK, CHUNK, "early1", last=True)
+
+        neg_max = [keep.tile([P, PACK], F32, name="neg_max%d" % h) for h in range(2)]
+        neg_top = keep.tile([P, PACK], F32, name="neg_top")
+        sums = [keep.tile([P, PACK], F32, name="sums%d" % h) for h in range(2)]
+        probs = keep.tile([P, PACK, I], F32, name="probs")
+        y = keep.tile([P, PACK, I], F32, name="y")
+
+        def row_max(h, pair):
+            nc.vector.tensor_reduce(
+                neg_max[h][:, 2 * pair:2 * pair + 2],
+                diff_banks[2 * h + pair][:].rearrange("p (r n) -> p r n", r=2),
+                AXIS_X, ALU.max, negate=True,
+            )
+
+        def exps(h, pair, neg_shift):
+            for r in range(2 * pair, 2 * pair + 2):
+                nc.scalar.activation(out=probs[:, r, h * HALF:(h + 1) * HALF], in_=score_view(h, r), func=ACT.Exp,
+                                     bias=neg_shift[:, r:r + 1], accum_out=sums[h][:, r:r + 1])
+
+        merge(0)
+        merge(1)
+        scores(0)
+        scores(1)
+        merge(2)
+        merge(3)
+        for pair in range(2):
+            row_max(0, pair)
+            exps(0, pair, neg_max[0])
+        scores(2)
+        scores(3)
+
+        gap = keep.tile([P, PACK], F32, name="gap")
+        carry = keep.tile([P, PACK], F32, name="carry")
+        carried = keep.tile([P, PACK], F32, name="carried")
+        total = keep.tile([P, PACK], F32, name="total")
+        inverse = keep.tile([P, PACK], F32, name="inverse")
+        out_v = out_0.rearrange("(p r) n -> p r n", r=PACK)
+        for pair in range(2):
+            two = slice(2 * pair, 2 * pair + 2)
+            row_max(1, pair)
+            nc.vector.tensor_tensor(neg_top[:, two], neg_max[0][:, two], neg_max[1][:, two], ALU.min)
+            exps(1, pair, neg_top)
+            nc.vector.tensor_tensor(gap[:, two], neg_top[:, two], neg_max[0][:, two], ALU.subtract)
+            nc.scalar.activation(out=carry[:, two], in_=gap[:, two], func=ACT.Exp)
+            nc.vector.scalar_tensor_tensor(carried[:, two], sums[0][:, two], 1.0 / I, carry[:, two], ALU.mult, ALU.mult)
+        for pair in range(2):
+            two = slice(2 * pair, 2 * pair + 2)
+            nc.vector.scalar_tensor_tensor(total[:, two], sums[1][:, two], 1.0 / I, carried[:, two], ALU.mult, ALU.add)
+            nc.vector.reciprocal(inverse[:, two], total[:, two])
+            for r in range(2 * pair, 2 * pair + 2):
+                nc.vector.tensor_scalar(y[:, r, 0:HALF], probs[:, r, 0:HALF], inverse[:, r:r + 1], carry[:, r:r + 1], ALU.mult, ALU.mult)
+                nc.scalar.activation(out=y[:, r, HALF:I], in_=probs[:, r, HALF:I], func=ACT.Copy, scale=inverse[:, r:r + 1])
+                nc.sync.dma_start(out=out_v[:, r, :], in_=y[:, r, :])
+
+        y_codes = keep.tile([P, I], U32, name="y_codes", align_bytes=64)
+        y_scales = keep.tile([P, I], U8, name="y_scales", align_bytes=64)
+        words = out_1.rearrange("z p c r -> p (z c r)").bitcast(I32)
+        for h in range(2):
+            cols = slice(h * HALF, (h + 1) * HALF)
+            y_bf = keep.tile([P, HALF, PACK], BF16, name="y_bf%d" % h, align_bytes=64)
+            nc.vector.tensor_copy(
+                y_bf[:].rearrange("p (a i) r -> p a r i", i=PACK),
+                y[:, :, cols].rearrange("p r (a i) -> p a r i", i=PACK),
+            )
+            nc.vector.quantize_mx(out=y_codes[:, cols].bitcast(FP8X4), scales=y_scales[:, cols], in_=y_bf[:].rearrange("p n r -> p (n r)"))
+            nc.sync.dma_start(out=words[:, cols], in_=y_codes[:, cols].bitcast(I32))
+        scale_rows = out_2.rearrange("z q c -> (z q) c").bitcast(I32)
+        for quad in range(4):
+            engine = nc.scalar if quad % 2 else nc.sync
+            engine.dma_start(out=scale_rows[4 * quad:4 * quad + 4, :], in_=y_scales[32 * quad:32 * quad + 4, :].bitcast(I32))

@@ -34,7 +34,7 @@ def tile_attend_similarmerge_pl_kernel(tc, query, keys, steep, th, dsc, offs, of
         offs_a = keep.tile([P, I // PER_COLUMN], U16, name="offs_a")
         offs_b = keep.tile([P, I // PER_COLUMN], U16, name="offs_b")
         planes = [keep.tile([P, T], F32, name="plane%d" % t) for t in range(PACK)]
-        q_raw = keep.tile([P, PACK, Q], F32, name="q_raw")
+        q_raw = [keep.tile([P, PACK, Q // 2], F32, name="q_raw%d" % h) for h in range(2)]
         dsc_t = keep.tile([P, PACK], F32, name="dsc_t")
         th_t = keep.tile([P, CHUNKS], F32, name="th_t")
         steep_t = keep.tile([P, CHUNKS], F32, name="steep_t")
@@ -44,8 +44,10 @@ def tile_attend_similarmerge_pl_kernel(tc, query, keys, steep, th, dsc, offs, of
         nc.sync.dma_start(offs_a[:], offs)
         nc.sync.dma_start(offs_b[:], offs2)
         nc.sync.dma_start(out=dsc_t[:], in_=dsc.rearrange("o (p t) -> p (o t)", t=PACK))
+        query_v = query.rearrange("(p t) n -> p t n", t=PACK)
+        nc.sync.dma_start(out=q_raw[0][:], in_=query_v[:, :, 0:Q // 2])
         nc.sync.dma_start(out=planes[1][:], in_=keys_v[:, 1, :])
-        nc.sync.dma_start(out=q_raw[:], in_=query.rearrange("(p t) n -> p t n", t=PACK))
+        nc.sync.dma_start(out=q_raw[1][:], in_=query_v[:, :, Q // 2:Q])
         nc.sync.dma_start(out=planes[2][:], in_=keys_v[:, 2, :])
         nc.sync.dma_start(out=planes[3][:], in_=keys_v[:, 3, :])
         with nc.allow_non_contiguous_dma(reason="one value a slot, slots on the partitions"):
@@ -66,21 +68,25 @@ def tile_attend_similarmerge_pl_kernel(tc, query, keys, steep, th, dsc, offs, of
         dot_banks = [psum.tile([P, PACK * P], F32, name="dot%d" % c) for c in range(CHUNKS)]
         planes_done = [0] * CHUNKS
 
-        def gather(t, first, count, tag, last=False):
-            cols = slice(first // PER_COLUMN, (first + count) // PER_COLUMN)
-            ka = keep.tile([P, count], F32, name="ka", tag="ka" + tag)
-            kb = keep.tile([P, count], F32, name="kb", tag="kb" + tag)
-            prod = keep.tile([P, count], F32, name="prod%d_%d" % (t, first))
-            kb_s = keep.tile([P, count], F32, name="kb_s%d_%d" % (t, first))
-            nc.vector.tensor_copy(ka[:], planes[t][:].indirect(offs_a[:, cols]))
-            nc.vector.tensor_copy(kb[:], planes[t][:].indirect(offs_b[:, cols]))
-            nc.scalar.activation(out=neg_ka[:, t, first:first + count], in_=ka[:], func=ACT.Copy, scale=neg_dsc[:, t:t + 1])
-            if last:
-                nc.vector.tensor_tensor(prod[:], ka[:], kb[:], ALU.mult)
-                nc.scalar.activation(out=kb_s[:], in_=kb[:], func=ACT.Copy, scale=dsc_t[:, t:t + 1])
+        def scale_by(who, out, in_, factor):
+            if who == "S":
+                nc.scalar.activation(out=out, in_=in_, func=ACT.Copy, scale=factor)
+            elif who == "V":
+                nc.vector.tensor_scalar(out, in_, factor, None, ALU.mult)
             else:
-                nc.gpsimd.tensor_tensor(prod[:], ka[:], kb[:], ALU.mult)
-                nc.gpsimd.tensor_scalar(kb_s[:], kb[:], dsc_t[:, t:t + 1], 0.0, ALU.mult, ALU.add)
+                nc.gpsimd.tensor_scalar(out, in_, factor, 0.0, ALU.mult, ALU.add)
+
+        def gather(t, first, count, who, tag=None, prod_tag=None):
+            cols = slice(first // PER_COLUMN, (first + count) // PER_COLUMN)
+            pair = keep.tile([P, 2 * count], F32, name="pair%d_%d" % (t, first), tag=tag or "pair%d_%d" % (t, first), align_bytes=64)
+            ka, kb = pair[:, 0:count], pair[:, count:2 * count]
+            prod = keep.tile([P, count], F32, name="prod%d_%d" % (t, first), tag="prod%d_%d" % (t, first), align_bytes=64)
+            kb_s = keep.tile([P, count], F32, name="kb_s%d_%d" % (t, first))
+            nc.vector.tensor_copy(ka, planes[t][:].indirect(offs_a[:, cols]))
+            nc.vector.tensor_copy(kb, planes[t][:].indirect(offs_b[:, cols]))
+            scale_by(who[0], neg_ka[:, t, first:first + count], ka, neg_dsc[:, t:t + 1])
+            (nc.vector if who[1] == "V" else nc.gpsimd).tensor_tensor(prod[:], ka, kb, ALU.mult)
+            scale_by(who[2], kb_s[:], kb, dsc_t[:, t:t + 1])
             for c in range(first // CHUNK, (first + count) // CHUNK):
                 here = slice(c * CHUNK - first, (c + 1) * CHUNK - first)
                 nc.tensor.matmul(dot_banks[c][:, 0:P], prod[:, here], ident[:], is_transpose=True,
@@ -94,29 +100,45 @@ def tile_attend_similarmerge_pl_kernel(tc, query, keys, steep, th, dsc, offs, of
         tanh_bias = keep.tile([P, CHUNKS], F32, name="tanh_bias")
         dot = keep.tile([P, CHUNKS], F32, name="dot")
         tanh_t = keep.tile([P, CHUNKS], F32, name="tanh_t")
-        share = keep.tile([P, CHUNKS], F32, name="share")
         k_codes = keep.tile([P, I], U32, name="k_codes", align_bytes=64)
         k_scales = keep.tile([P, I], U8, name="k_scales", align_bytes=64)
         q_codes = keep.tile([P, Q], U32, name="q_codes", align_bytes=64)
-        q_scales = keep.tile([P, Q], U8, name="q_scales", align_bytes=64)
 
-        def quantise_query():
-            q_bf = keep.tile([P, PACK, P, PACK], BF16, name="q_bf", align_bytes=64)
-            for s0 in range(0, P, 32):
+        q_bf = keep.tile([P, PACK, P, PACK], BF16, name="q_bf", align_bytes=64)
+
+        def round_query(h):
+            for part in range(2):
+                s0 = 32 * part
                 nc.scalar.copy(
-                    out=q_bf[:, :, s0:s0 + 32, :].rearrange("p r s t -> p s t r"),
-                    in_=q_raw[:, :, PACK * s0:PACK * (s0 + 32)].rearrange("p t (s r) -> p s t r", r=PACK),
+                    out=q_bf[:, :, 64 * h + s0:64 * h + s0 + 32, :].rearrange("p r s t -> p s t r"),
+                    in_=q_raw[h][:, :, PACK * s0:PACK * (s0 + 32)].rearrange("p t (s r) -> p s t r", r=PACK),
                 )
-            nc.vector.quantize_mx(out=q_codes[:].bitcast(FP8X4), scales=q_scales[:], in_=q_bf[:].rearrange("p r s t -> p (r s t)"))
+
+        steps = [keep.tile([P, PACK * P], F32, name="step%d" % c) for c in range(CHUNKS)]
+
+        def weigh(chunks, who, step_who):
+            cols = slice(chunks[0], chunks[-1] + 1)
+            for c, w in zip(chunks, who):
+                if w == "S":
+                    spent = keep.tile([P, P], F32, name="spent%d" % c, tag="spent%d" % c, align_bytes=64)
+                    nc.scalar.activation(out=spent[:], in_=dot_banks[c][:, 0:P], func=ACT.Copy, accum_out=dot[:, c:c + 1])
+                else:
+                    nc.vector.tensor_reduce(dot[:, c:c + 1], dot_banks[c][:, 0:P], AXIS_X, ALU.add)
+            share = keep.tile([P, len(chunks)], F32, name="share%d" % chunks[0], tag="share%d" % chunks[0], align_bytes=64)
+            if len(chunks) == 1:
+                nc.scalar.activation(out=tanh_t[:, cols], in_=dot[:, cols], func=ACT.Tanh, scale=tanh_scale[:, cols], bias=tanh_bias[:, cols])
+            else:
+                for c in chunks:
+                    nc.scalar.activation(out=tanh_t[:, c:c + 1], in_=dot[:, c:c + 1], func=ACT.Tanh, scale=tanh_scale[:, c:c + 1], bias=tanh_bias[:, c:c + 1])
+            nc.scalar.activation(out=share[:], in_=tanh_t[:, cols], func=ACT.Copy, scale=0.25, bias=0.25)
+            for n, c in enumerate(chunks):
+                if step_who[n] == "S":
+                    nc.scalar.activation(out=steps[c][:], in_=diff_banks[c][:], func=ACT.Copy, scale=share[:, n:n + 1])
+                else:
+                    nc.vector.tensor_scalar(steps[c][:], diff_banks[c][:], share[:, n:n + 1], None, ALU.mult)
 
         def merge(c):
-            col = slice(c, c + 1)
-            spent = keep.tile([P, P], F32, name="spent%d" % c)
-            nc.scalar.activation(out=spent[:], in_=dot_banks[c][:, 0:P], func=ACT.Copy, accum_out=dot[:, col])
-            nc.scalar.activation(out=tanh_t[:, col], in_=dot[:, col], func=ACT.Tanh, scale=tanh_scale[:, col], bias=tanh_bias[:, col])
-            nc.scalar.activation(out=share[:, col], in_=tanh_t[:, col], func=ACT.Copy, scale=0.25, bias=0.25)
-            step = keep.tile([P, PACK * P], F32, name="step%d" % c)
-            nc.scalar.activation(out=step[:], in_=diff_banks[c][:], func=ACT.Copy, scale=share[:, col])
+            step = steps[c]
             for t in range(PACK):
                 nc.tensor.transpose(dot_banks[c][:, t * P:(t + 1) * P], step[:, t * P:(t + 1) * P], ident[:])
             km = keep.tile([P, CHUNK, PACK], BF16, name="km%d" % c, align_bytes=64)
@@ -129,97 +151,77 @@ def tile_attend_similarmerge_pl_kernel(tc, query, keys, steep, th, dsc, offs, of
             slots = slice(c * CHUNK, (c + 1) * CHUNK)
             nc.vector.quantize_mx(out=k_codes[:, slots].bitcast(FP8X4), scales=k_scales[:, slots], in_=km[:].rearrange("p n t -> p (n t)"))
 
-        def score_view(h, r):
-            return diff_banks[2 * h + r // 2][:, (r % 2) * HALF:(r % 2 + 1) * HALF]
+        score_banks = [diff_banks[0], diff_banks[1], dot_banks[0], dot_banks[1]]
 
-        def scores(c):
-            slots = slice(c * CHUNK, (c + 1) * CHUNK)
+        def scores(first, count):
+            slots = slice(first, first + count)
             for r in range(PACK):
                 rows = slice(r * P, (r + 1) * P)
                 nc.tensor.matmul_mx(
-                    out=score_view(c // 2, r)[:, (c % 2) * CHUNK:(c % 2 + 1) * CHUNK],
+                    out=score_banks[r][:, slots],
                     lhsT=q_codes[:, rows].bitcast(FP8X4), lhsT_scale=q_scales[:, rows],
                     rhs=k_codes[:, slots].bitcast(FP8X4), rhs_scale=k_scales[:, slots],
                     start=True, stop=True,
                 )
 
-        gather(0, 0, I, "0")
-        gather(1, 0, I, "1")
-        quantise_query()
-        gather(2, 0, HALF, "2")
-        nc.gpsimd.tensor_scalar(tanh_scale[:], steep_t[:], 0.5 / D, 0.0, ALU.mult, ALU.add)
-        nc.gpsimd.tensor_tensor(tanh_bias[:], th_t[:], steep_t[:], ALU.mult)
-        nc.gpsimd.tensor_scalar(tanh_bias[:], tanh_bias[:], -0.5, 0.0, ALU.mult, ALU.add)
-        gather(3, 0, CHUNK, "early0")
-        gather(3, CHUNK, CHUNK, "early1")
-        gather(3, HALF, HALF, "3")
-        gather(2, 2 * CHUNK, CHUNK, "early0", last=True)
-        gather(2, 3 * CHUNK, CHUNK, "early1", last=True)
-
-        neg_max = [keep.tile([P, PACK], F32, name="neg_max%d" % h) for h in range(2)]
-        neg_top = keep.tile([P, PACK], F32, name="neg_top")
-        sums = [keep.tile([P, PACK], F32, name="sums%d" % h) for h in range(2)]
-        probs = keep.tile([P, PACK, I], F32, name="probs")
-        y = keep.tile([P, PACK, I], F32, name="y")
-
-        def row_max(h, pair):
-            nc.vector.tensor_reduce(
-                neg_max[h][:, 2 * pair:2 * pair + 2],
-                diff_banks[2 * h + pair][:].rearrange("p (r n) -> p r n", r=2),
-                AXIS_X, ALU.max, negate=True,
-            )
-
-        def exps(h, pair, neg_shift):
-            for r in range(2 * pair, 2 * pair + 2):
-                nc.scalar.activation(out=probs[:, r, h * HALF:(h + 1) * HALF], in_=score_view(h, r), func=ACT.Exp,
-                                     bias=neg_shift[:, r:r + 1], accum_out=sums[h][:, r:r + 1])
+        gather(0, 0, I, "SGG")
+        round_query(0)
+        gather(1, 0, I, "SGG")
+        round_query(1)
+        gather(2, 0, HALF, "SGS")
+        gather(2, HALF, HALF, "SGS")
+        nc.scalar.activation(out=tanh_scale[:], in_=steep_t[:], func=ACT.Copy, scale=0.5 / D)
+        nc.vector.scalar_tensor_tensor(tanh_bias[:], th_t[:], -0.5, steep_t[:], ALU.mult, ALU.mult)
+        gather(3, 0 * CHUNK, CHUNK, "SVS")
+        gather(3, 1 * CHUNK, CHUNK, "SVS")
+        gather(3, 2 * CHUNK, CHUNK, "VVV")
+        gather(3, 3 * CHUNK, CHUNK, "VVV")
+        q_scales = keep.tile([P, Q], U8, name="q_scales", tag="pair3_128", align_bytes=64)
+        nc.vector.quantize_mx(out=q_codes[:].bitcast(FP8X4), scales=q_scales[:], in_=q_bf[:].rearrange("p r s t -> p (r s t)"))
+        weigh([0], "S", "S")
+        weigh([1], "S", "V")
+        weigh([2], "S", "S")
+        weigh([3], "S", "S")
 
         merge(0)
         merge(1)
-        scores(0)
-        scores(1)
         merge(2)
         merge(3)
-        for pair in range(2):
-            row_max(0, pair)
-            exps(0, pair, neg_max[0])
-        scores(2)
-        scores(3)
+        scores(0, HALF)
+        scores(HALF, HALF)
 
-        gap = keep.tile([P, PACK], F32, name="gap")
-        carry = keep.tile([P, PACK], F32, name="carry")
-        carried = keep.tile([P, PACK], F32, name="carried")
-        total = keep.tile([P, PACK], F32, name="total")
+        neg_max = keep.tile([P, PACK], F32, name="neg_max")
+        sums = keep.tile([P, PACK], F32, name="sums")
         inverse = keep.tile([P, PACK], F32, name="inverse")
-        out_v = out_0.rearrange("(p r) n -> p r n", r=PACK)
-        for pair in range(2):
-            two = slice(2 * pair, 2 * pair + 2)
-            row_max(1, pair)
-            nc.vector.tensor_tensor(neg_top[:, two], neg_max[0][:, two], neg_max[1][:, two], ALU.min)
-            exps(1, pair, neg_top)
-            nc.vector.tensor_tensor(gap[:, two], neg_top[:, two], neg_max[0][:, two], ALU.subtract)
-            nc.scalar.activation(out=carry[:, two], in_=gap[:, two], func=ACT.Exp)
-            nc.vector.scalar_tensor_tensor(carried[:, two], sums[0][:, two], 1.0 / I, carry[:, two], ALU.mult, ALU.mult)
-        for pair in range(2):
-            two = slice(2 * pair, 2 * pair + 2)
-            nc.vector.scalar_tensor_tensor(total[:, two], sums[1][:, two], 1.0 / I, carried[:, two], ALU.mult, ALU.add)
-            nc.vector.reciprocal(inverse[:, two], total[:, two])
-            for r in range(2 * pair, 2 * pair + 2):
-                nc.vector.tensor_scalar(y[:, r, 0:HALF], probs[:, r, 0:HALF], inverse[:, r:r + 1], carry[:, r:r + 1], ALU.mult, ALU.mult)
-                nc.scalar.activation(out=y[:, r, HALF:I], in_=probs[:, r, HALF:I], func=ACT.Copy, scale=inverse[:, r:r + 1])
-                nc.sync.dma_start(out=out_v[:, r, :], in_=y[:, r, :])
-
+        probs = keep.tile([P, PACK, I], F32, name="probs")
+        y = keep.tile([P, PACK, I], F32, name="y")
         y_codes = keep.tile([P, I], U32, name="y_codes", align_bytes=64)
         y_scales = keep.tile([P, I], U8, name="y_scales", align_bytes=64)
+        y_bf = keep.tile([P, I, PACK], BF16, name="y_bf", align_bytes=64)
+        out_v = out_0.rearrange("(p r) n -> p r n", r=PACK)
         words = out_1.rearrange("z p c r -> p (z c r)").bitcast(I32)
+
+        def round_pair(pair, cols):
+            two = slice(2 * pair, 2 * pair + 2)
+            nc.vector.tensor_copy(
+                y_bf[:, cols, two].rearrange("p (a i) r -> p a r i", i=PACK),
+                y[:, two, cols].rearrange("p r (a i) -> p a r i", i=PACK),
+            )
+
+        for r in range(PACK):
+            nc.vector.tensor_reduce(neg_max[:, r:r + 1], score_banks[r][:], AXIS_X, ALU.max, negate=True)
+            nc.scalar.activation(out=probs[:, r, :], in_=score_banks[r][:], func=ACT.Exp, bias=neg_max[:, r:r + 1], accum_out=sums[:, r:r + 1])
+        for r in range(PACK):
+            nc.vector.reciprocal(inverse[:, r:r + 1], sums[:, r:r + 1])
+            nc.vector.tensor_scalar(y[:, r, :], probs[:, r, :], inverse[:, r:r + 1], float(I), ALU.mult, ALU.mult)
+            nc.sync.dma_start(out=out_v[:, r, :], in_=y[:, r, :])
+            if r == 1:
+                round_pair(0, slice(0, I))
+
         for h in range(2):
             cols = slice(h * HALF, (h + 1) * HALF)
-            y_bf = keep.tile([P, HALF, PACK], BF16, name="y_bf%d" % h, align_bytes=64)
-            nc.vector.tensor_copy(
-                y_bf[:].rearrange("p (a i) r -> p a r i", i=PACK),
-                y[:, :, cols].rearrange("p r (a i) -> p a r i", i=PACK),
-            )
-            nc.vector.quantize_mx(out=y_codes[:, cols].bitcast(FP8X4), scales=y_scales[:, cols], in_=y_bf[:].rearrange("p n r -> p (n r)"))
+            round_pair(1, cols)
+            nc.vector.quantize_mx(out=y_codes[:, cols].bitcast(FP8X4), scales=y_scales[:, cols], in_=y_bf[:, cols, :].rearrange("p n r -> p (n r)"))
             nc.sync.dma_start(out=words[:, cols], in_=y_codes[:, cols].bitcast(I32))
         scale_rows = out_2.rearrange("z q c -> (z q) c").bitcast(I32)
         for quad in range(4):

@@ -21,6 +21,9 @@ CHUNK = 128
 CHUNKS = I // CHUNK
 HALF = I // 2
 PER_COLUMN = 16
+RUN = 4
+ROUND_STEP = 32
+QUADRANT = 32
 
 FLOPS = 2 * D * I * Q
 
@@ -40,11 +43,11 @@ def tile_attend_similarmerge_pl_kernel(tc, query, keys, steep, th, dsc, offs, of
         steep_t = keep.tile([P, CHUNKS], F32, name="steep_t")
 
         keys_v = keys.rearrange("(p t) n -> p t n", t=PACK)
+        query_v = query.rearrange("(p t) n -> p t n", t=PACK)
         nc.sync.dma_start(out=planes[0][:], in_=keys_v[:, 0, :])
         nc.sync.dma_start(offs_a[:], offs)
         nc.sync.dma_start(offs_b[:], offs2)
         nc.sync.dma_start(out=dsc_t[:], in_=dsc.rearrange("o (p t) -> p (o t)", t=PACK))
-        query_v = query.rearrange("(p t) n -> p t n", t=PACK)
         nc.sync.dma_start(out=q_raw[0][:], in_=query_v[:, :, 0:Q // 2])
         nc.sync.dma_start(out=planes[1][:], in_=keys_v[:, 1, :])
         nc.sync.dma_start(out=q_raw[1][:], in_=query_v[:, :, Q // 2:Q])
@@ -64,97 +67,124 @@ def tile_attend_similarmerge_pl_kernel(tc, query, keys, steep, th, dsc, offs, of
         nc.scalar.activation(out=neg_dsc[:], in_=dsc_t[:], func=ACT.Copy, scale=-1.0)
 
         neg_ka = keep.tile([P, PACK, I], F32, name="neg_ka")
-        diff_banks = [psum.tile([P, PACK * P], F32, name="diff%d" % c) for c in range(CHUNKS)]
+        diff = keep.tile([P, PACK, HALF], F32, name="diff")
         dot_banks = [psum.tile([P, PACK * P], F32, name="dot%d" % c) for c in range(CHUNKS)]
-        planes_done = [0] * CHUNKS
+        move_banks = [psum.tile([P, PACK * P], F32, name="move%d" % c) for c in range(CHUNKS)]
+        spread_bank = move_banks[0]
 
-        def scale_by(who, out, in_, factor):
-            if who == "S":
-                nc.scalar.activation(out=out, in_=in_, func=ACT.Copy, scale=factor)
-            elif who == "V":
+        def scale_rows(on_vector, out, in_, factor):
+            if on_vector:
                 nc.vector.tensor_scalar(out, in_, factor, None, ALU.mult)
             else:
-                nc.gpsimd.tensor_scalar(out, in_, factor, 0.0, ALU.mult, ALU.add)
+                nc.scalar.activation(out=out, in_=in_, func=ACT.Copy, scale=factor)
 
-        def gather(t, first, count, who, tag=None, prod_tag=None):
+        def gather(t, first, count, two_input, scale_on_vector=False):
             cols = slice(first // PER_COLUMN, (first + count) // PER_COLUMN)
-            pair = keep.tile([P, 2 * count], F32, name="pair%d_%d" % (t, first), tag=tag or "pair%d_%d" % (t, first), align_bytes=64)
+            piece = "%d_%d" % (t, first)
+            pair = keep.tile([P, 2 * count], F32, name="pair" + piece, tag="pair" + piece, align_bytes=64)
             ka, kb = pair[:, 0:count], pair[:, count:2 * count]
-            prod = keep.tile([P, count], F32, name="prod%d_%d" % (t, first), tag="prod%d_%d" % (t, first), align_bytes=64)
-            kb_s = keep.tile([P, count], F32, name="kb_s%d_%d" % (t, first))
             nc.vector.tensor_copy(ka, planes[t][:].indirect(offs_a[:, cols]))
             nc.vector.tensor_copy(kb, planes[t][:].indirect(offs_b[:, cols]))
-            scale_by(who[0], neg_ka[:, t, first:first + count], ka, neg_dsc[:, t:t + 1])
-            (nc.vector if who[1] == "V" else nc.gpsimd).tensor_tensor(prod[:], ka, kb, ALU.mult)
-            scale_by(who[2], kb_s[:], kb, dsc_t[:, t:t + 1])
+            scale_rows(scale_on_vector, neg_ka[:, t, first:first + count], ka, neg_dsc[:, t:t + 1])
+            prod = keep.tile([P, count], F32, name="prod" + piece)
+            two_input.tensor_tensor(prod[:], ka, kb, ALU.mult)
+            spread = min(max(HALF - first, 0), count)
+            if spread < count:
+                kb_s = keep.tile([P, count], F32, name="kb_s" + piece)
+                scale_rows(scale_on_vector, kb_s[:, spread:count], kb[:, spread:count], dsc_t[:, t:t + 1])
+            if spread > 0:
+                two_input.tensor_tensor(diff[:, t, first:first + spread], kb[:, 0:spread], ka[:, 0:spread], ALU.subtract)
             for c in range(first // CHUNK, (first + count) // CHUNK):
                 here = slice(c * CHUNK - first, (c + 1) * CHUNK - first)
                 nc.tensor.matmul(dot_banks[c][:, 0:P], prod[:, here], ident[:], is_transpose=True,
-                                 start=planes_done[c] == 0, stop=planes_done[c] == PACK - 1)
-                target = diff_banks[c][:, t * P:(t + 1) * P]
-                nc.tensor.matmul(target, neg_ka[:, t, c * CHUNK:(c + 1) * CHUNK], ident[:], is_transpose=True, start=True, stop=False)
-                nc.tensor.matmul(target, kb_s[:, here], ident[:], is_transpose=True, start=False, stop=True)
-                planes_done[c] = planes_done[c] + 1
-
-        tanh_scale = keep.tile([P, CHUNKS], F32, name="tanh_scale")
-        tanh_bias = keep.tile([P, CHUNKS], F32, name="tanh_bias")
-        dot = keep.tile([P, CHUNKS], F32, name="dot")
-        tanh_t = keep.tile([P, CHUNKS], F32, name="tanh_t")
-        k_codes = keep.tile([P, I], U32, name="k_codes", align_bytes=64)
-        k_scales = keep.tile([P, I], U8, name="k_scales", align_bytes=64)
-        q_codes = keep.tile([P, Q], U32, name="q_codes", align_bytes=64)
+                                 start=t == 0, stop=t == PACK - 1)
+                if c * CHUNK >= HALF:
+                    target = move_banks[c][:, t * P:(t + 1) * P]
+                    nc.tensor.matmul(target, neg_ka[:, t, c * CHUNK:(c + 1) * CHUNK], ident[:], is_transpose=True,
+                                     start=True, stop=False)
+                    nc.tensor.matmul(target, kb_s[:, here], ident[:], is_transpose=True, start=False, stop=True)
 
         q_bf = keep.tile([P, PACK, P, PACK], BF16, name="q_bf", align_bytes=64)
 
         def round_query(h):
-            for part in range(2):
-                s0 = 32 * part
+            for s0 in range(0, P // 2, ROUND_STEP):
+                place = h * P // 2 + s0
                 nc.scalar.copy(
-                    out=q_bf[:, :, 64 * h + s0:64 * h + s0 + 32, :].rearrange("p r s t -> p s t r"),
-                    in_=q_raw[h][:, :, PACK * s0:PACK * (s0 + 32)].rearrange("p t (s r) -> p s t r", r=PACK),
+                    out=q_bf[:, :, place:place + ROUND_STEP, :].rearrange("p r s t -> p s t r"),
+                    in_=q_raw[h][:, :, PACK * s0:PACK * (s0 + ROUND_STEP)].rearrange("p t (s r) -> p s t r", r=PACK),
                 )
 
-        steps = [keep.tile([P, PACK * P], F32, name="step%d" % c) for c in range(CHUNKS)]
+        gather(0, 0, I, nc.gpsimd)
+        round_query(0)
+        gather(1, 0, I, nc.gpsimd)
+        round_query(1)
+        gather(2, 0, HALF, nc.gpsimd)
+        gather(2, HALF, HALF, nc.vector)
+        tanh_scale = keep.tile([P, CHUNKS], F32, name="tanh_scale")
+        term_bias = keep.tile([P, CHUNKS], F32, name="term_bias")
+        nc.scalar.activation(out=tanh_scale[:], in_=steep_t[:], func=ACT.Copy, scale=0.5 / D)
+        nc.scalar.activation(out=term_bias[:], in_=th_t[:], func=ACT.Copy, scale=-float(D // P))
+        for c in range(CHUNKS):
+            gather(PACK - 1, c * CHUNK, CHUNK, nc.vector, scale_on_vector=c * CHUNK >= HALF)
 
-        def weigh(chunks, who, step_who):
-            cols = slice(chunks[0], chunks[-1] + 1)
-            for c, w in zip(chunks, who):
-                if w == "S":
-                    spent = keep.tile([P, P], F32, name="spent%d" % c, tag="spent%d" % c, align_bytes=64)
-                    nc.scalar.activation(out=spent[:], in_=dot_banks[c][:, 0:P], func=ACT.Copy, accum_out=dot[:, c:c + 1])
-                else:
-                    nc.vector.tensor_reduce(dot[:, c:c + 1], dot_banks[c][:, 0:P], AXIS_X, ALU.add)
-            share = keep.tile([P, len(chunks)], F32, name="share%d" % chunks[0], tag="share%d" % chunks[0], align_bytes=64)
-            if len(chunks) == 1:
-                nc.scalar.activation(out=tanh_t[:, cols], in_=dot[:, cols], func=ACT.Tanh, scale=tanh_scale[:, cols], bias=tanh_bias[:, cols])
+        q_codes = keep.tile([P, Q], U32, name="q_codes", align_bytes=64)
+        q_scales = keep.tile([P, Q], U8, name="q_scales", tag="pair%d_%d" % (PACK - 1, CHUNK), align_bytes=64)
+        nc.vector.quantize_mx(out=q_codes[:].bitcast(FP8X4), scales=q_scales[:],
+                              in_=q_bf[:].rearrange("p r s t -> p (r s t)"))
+
+        centred = keep.tile([P, CHUNKS], F32, name="centred")
+
+        def weigh(c):
+            col = slice(c, c + 1)
+            turned = c * CHUNK >= HALF
+            terms = keep.tile([P, P], F32, name="terms%d" % c, tag="tanh%d" % (c - 1) if turned else "terms%d" % c)
+            nc.scalar.activation(out=terms[:], in_=dot_banks[c][:, 0:P], func=ACT.Identity, bias=term_bias[:, col],
+                                 accum_out=centred[:, col])
+            tanh_c = keep.tile([P, 1], F32, name="tanh%d" % c, tag="tanh%d" % c)
+            nc.scalar.activation(out=tanh_c[:], in_=centred[:, col], func=ACT.Tanh, scale=tanh_scale[:, col])
+            if turned:
+                share = keep.tile([P, 1], F32, name="share%d" % c)
+                nc.scalar.activation(out=share[:], in_=tanh_c[:], func=ACT.Copy, scale=0.25, bias=0.25)
+                step = keep.tile([P, PACK * P], F32, name="step%d" % c)
+                nc.scalar.activation(out=step[:], in_=move_banks[c][:], func=ACT.Copy, scale=share[:])
+                for t in range(PACK):
+                    nc.tensor.transpose(dot_banks[c][:, t * P:(t + 1) * P], step[:, t * P:(t + 1) * P], ident[:])
             else:
-                for c in chunks:
-                    nc.scalar.activation(out=tanh_t[:, c:c + 1], in_=dot[:, c:c + 1], func=ACT.Tanh, scale=tanh_scale[:, c:c + 1], bias=tanh_bias[:, c:c + 1])
-            nc.scalar.activation(out=share[:], in_=tanh_t[:, cols], func=ACT.Copy, scale=0.25, bias=0.25)
-            for n, c in enumerate(chunks):
-                if step_who[n] == "S":
-                    nc.scalar.activation(out=steps[c][:], in_=diff_banks[c][:], func=ACT.Copy, scale=share[:, n:n + 1])
-                else:
-                    nc.vector.tensor_scalar(steps[c][:], diff_banks[c][:], share[:, n:n + 1], None, ALU.mult)
+                share = keep.tile([P, P], F32, name="share%d" % c)
+                nc.scalar.activation(out=share[:], in_=tanh_c[:].to_broadcast([P, P]), func=ACT.Copy, scale=0.25, bias=0.25)
+                nc.tensor.transpose(spread_bank[:, c * CHUNK:(c + 1) * CHUNK], share[:], ident[:])
+
+        k_codes = keep.tile([P, I], U32, name="k_codes", align_bytes=64)
+        k_scales = keep.tile([P, I], U8, name="k_scales", align_bytes=64)
 
         def merge(c):
-            step = steps[c]
-            for t in range(PACK):
-                nc.tensor.transpose(dot_banks[c][:, t * P:(t + 1) * P], step[:, t * P:(t + 1) * P], ident[:])
+            slots = slice(c * CHUNK, (c + 1) * CHUNK)
+            if c * CHUNK >= HALF:
+                moved = dot_banks[c][:].rearrange("p (t n) -> p t n", t=PACK)
+            else:
+                moved = spread_moved[:, :, slots]
             km = keep.tile([P, CHUNK, PACK], BF16, name="km%d" % c, align_bytes=64)
             nc.vector.tensor_tensor(
-                km[:].rearrange("p (a i) t -> p a t i", i=PACK),
-                dot_banks[c][:].rearrange("p (t a i) -> p a t i", t=PACK, i=PACK),
-                neg_ka[:, :, c * CHUNK:(c + 1) * CHUNK].rearrange("p t (a i) -> p a t i", i=PACK),
+                km[:].rearrange("p (a i) t -> p a t i", i=RUN),
+                moved.rearrange("p t (a i) -> p a t i", i=RUN),
+                neg_ka[:, :, slots].rearrange("p t (a i) -> p a t i", i=RUN),
                 ALU.subtract,
             )
-            slots = slice(c * CHUNK, (c + 1) * CHUNK)
-            nc.vector.quantize_mx(out=k_codes[:, slots].bitcast(FP8X4), scales=k_scales[:, slots], in_=km[:].rearrange("p n t -> p (n t)"))
+            nc.vector.quantize_mx(out=k_codes[:, slots].bitcast(FP8X4), scales=k_scales[:, slots],
+                                  in_=km[:].rearrange("p n t -> p (n t)"))
 
-        score_banks = [diff_banks[0], diff_banks[1], dot_banks[0], dot_banks[1]]
+        for c in range(CHUNKS):
+            weigh(c)
+        spread_moved = keep.tile([P, PACK, HALF], F32, name="spread_moved")
+        for t in range(PACK):
+            nc.vector.scalar_tensor_tensor(spread_moved[:, t, :], diff[:, t, :], dsc_t[:, t:t + 1],
+                                           spread_bank[:, 0:HALF], ALU.mult, ALU.mult)
+        for c in range(CHUNKS):
+            merge(c)
 
-        def scores(first, count):
-            slots = slice(first, first + count)
+        score_banks = [move_banks[1], dot_banks[0], dot_banks[1], move_banks[0]]
+        for first in range(0, I, HALF):
+            slots = slice(first, first + HALF)
             for r in range(PACK):
                 rows = slice(r * P, (r + 1) * P)
                 nc.tensor.matmul_mx(
@@ -164,53 +194,25 @@ def tile_attend_similarmerge_pl_kernel(tc, query, keys, steep, th, dsc, offs, of
                     start=True, stop=True,
                 )
 
-        gather(0, 0, I, "SGG")
-        round_query(0)
-        gather(1, 0, I, "SGG")
-        round_query(1)
-        gather(2, 0, HALF, "SGS")
-        gather(2, HALF, HALF, "SGS")
-        nc.scalar.activation(out=tanh_scale[:], in_=steep_t[:], func=ACT.Copy, scale=0.5 / D)
-        nc.vector.scalar_tensor_tensor(tanh_bias[:], th_t[:], -0.5, steep_t[:], ALU.mult, ALU.mult)
-        gather(3, 0 * CHUNK, CHUNK, "SVS")
-        gather(3, 1 * CHUNK, CHUNK, "SVS")
-        gather(3, 2 * CHUNK, CHUNK, "VVV")
-        gather(3, 3 * CHUNK, CHUNK, "VVV")
-        q_scales = keep.tile([P, Q], U8, name="q_scales", tag="pair3_128", align_bytes=64)
-        nc.vector.quantize_mx(out=q_codes[:].bitcast(FP8X4), scales=q_scales[:], in_=q_bf[:].rearrange("p r s t -> p (r s t)"))
-        weigh([0], "S", "S")
-        weigh([1], "S", "V")
-        weigh([2], "S", "S")
-        weigh([3], "S", "S")
-
-        merge(0)
-        merge(1)
-        merge(2)
-        merge(3)
-        scores(0, HALF)
-        scores(HALF, HALF)
-
         neg_max = keep.tile([P, PACK], F32, name="neg_max")
         sums = keep.tile([P, PACK], F32, name="sums")
         inverse = keep.tile([P, PACK], F32, name="inverse")
         probs = keep.tile([P, PACK, I], F32, name="probs")
         y = keep.tile([P, PACK, I], F32, name="y")
-        y_codes = keep.tile([P, I], U32, name="y_codes", align_bytes=64)
-        y_scales = keep.tile([P, I], U8, name="y_scales", align_bytes=64)
         y_bf = keep.tile([P, I, PACK], BF16, name="y_bf", align_bytes=64)
         out_v = out_0.rearrange("(p r) n -> p r n", r=PACK)
-        words = out_1.rearrange("z p c r -> p (z c r)").bitcast(I32)
 
         def round_pair(pair, cols):
             two = slice(2 * pair, 2 * pair + 2)
             nc.vector.tensor_copy(
-                y_bf[:, cols, two].rearrange("p (a i) r -> p a r i", i=PACK),
-                y[:, two, cols].rearrange("p r (a i) -> p a r i", i=PACK),
+                y_bf[:, cols, two].rearrange("p (a i) r -> p a r i", i=RUN),
+                y[:, two, cols].rearrange("p r (a i) -> p a r i", i=RUN),
             )
 
         for r in range(PACK):
             nc.vector.tensor_reduce(neg_max[:, r:r + 1], score_banks[r][:], AXIS_X, ALU.max, negate=True)
-            nc.scalar.activation(out=probs[:, r, :], in_=score_banks[r][:], func=ACT.Exp, bias=neg_max[:, r:r + 1], accum_out=sums[:, r:r + 1])
+            nc.scalar.activation(out=probs[:, r, :], in_=score_banks[r][:], func=ACT.Exp, bias=neg_max[:, r:r + 1],
+                                 accum_out=sums[:, r:r + 1])
         for r in range(PACK):
             nc.vector.reciprocal(inverse[:, r:r + 1], sums[:, r:r + 1])
             nc.vector.tensor_scalar(y[:, r, :], probs[:, r, :], inverse[:, r:r + 1], float(I), ALU.mult, ALU.mult)
@@ -218,12 +220,16 @@ def tile_attend_similarmerge_pl_kernel(tc, query, keys, steep, th, dsc, offs, of
             if r == 1:
                 round_pair(0, slice(0, I))
 
-        for h in range(2):
+        y_codes = keep.tile([P, I], U32, name="y_codes", align_bytes=64)
+        y_scales = keep.tile([P, I], U8, name="y_scales", align_bytes=64)
+        words = out_1.rearrange("z p c r -> p (z c r)").bitcast(I32)
+        for h, queue in enumerate((nc.sync, nc.scalar)):
             cols = slice(h * HALF, (h + 1) * HALF)
             round_pair(1, cols)
-            nc.vector.quantize_mx(out=y_codes[:, cols].bitcast(FP8X4), scales=y_scales[:, cols], in_=y_bf[:, cols, :].rearrange("p n r -> p (n r)"))
-            nc.sync.dma_start(out=words[:, cols], in_=y_codes[:, cols].bitcast(I32))
-        scale_rows = out_2.rearrange("z q c -> (z q) c").bitcast(I32)
-        for quad in range(4):
-            engine = nc.scalar if quad % 2 else nc.sync
-            engine.dma_start(out=scale_rows[4 * quad:4 * quad + 4, :], in_=y_scales[32 * quad:32 * quad + 4, :].bitcast(I32))
+            nc.vector.quantize_mx(out=y_codes[:, cols].bitcast(FP8X4), scales=y_scales[:, cols],
+                                  in_=y_bf[:, cols, :].rearrange("p n r -> p (n r)"))
+            queue.dma_start(out=words[:, cols], in_=y_codes[:, cols].bitcast(I32))
+        scale_rows_out = out_2.rearrange("z q c -> (z q) c").bitcast(I32)
+        for j, queue in enumerate((nc.sync, nc.sync, nc.sync, nc.scalar)):
+            queue.dma_start(out=scale_rows_out[PACK * j:PACK * (j + 1), :],
+                            in_=y_scales[QUADRANT * j:QUADRANT * j + PACK, :].bitcast(I32))

@@ -24,6 +24,8 @@ PER_COLUMN = 16
 RUN = 4
 ROUND_STEP = 32
 QUADRANT = 32
+SCALE_ROWS = 4
+OUT_SCALE = 512.0
 
 FLOPS = 2 * D * I * Q
 
@@ -39,8 +41,10 @@ def tile_attend_similarmerge_pl_kernel(tc, query, keys, steep, th, dsc, offs, of
         planes = [keep.tile([P, T], F32, name="plane%d" % t) for t in range(PACK)]
         q_raw = [keep.tile([P, PACK, Q // 2], F32, name="q_raw%d" % h) for h in range(2)]
         dsc_t = keep.tile([P, PACK], F32, name="dsc_t")
-        th_t = keep.tile([P, CHUNKS], F32, name="th_t")
-        steep_t = keep.tile([P, CHUNKS], F32, name="steep_t")
+        slot_rows = keep.tile([P, P], F32, name="slot_rows")
+        nc.gpsimd.memset(slot_rows[:], 0.0)
+        nc.scalar.dma_start(out=slot_rows[0:CHUNKS, :], in_=th.rearrange("(c p) o -> c (p o)", p=P))
+        nc.scalar.dma_start(out=slot_rows[CHUNKS:2 * CHUNKS, :], in_=steep.rearrange("(c p) o -> c (p o)", p=P))
 
         keys_v = keys.rearrange("(p t) n -> p t n", t=PACK)
         query_v = query.rearrange("(p t) n -> p t n", t=PACK)
@@ -53,15 +57,9 @@ def tile_attend_similarmerge_pl_kernel(tc, query, keys, steep, th, dsc, offs, of
         nc.sync.dma_start(out=q_raw[1][:], in_=query_v[:, :, Q // 2:Q])
         nc.sync.dma_start(out=planes[2][:], in_=keys_v[:, 2, :])
         nc.sync.dma_start(out=planes[3][:], in_=keys_v[:, 3, :])
-        with nc.allow_non_contiguous_dma(reason="one value a slot, slots on the partitions"):
-            nc.sync.dma_start(out=th_t[:], in_=th.rearrange("(c p) o -> p (c o)", p=P))
-            nc.sync.dma_start(out=steep_t[:], in_=steep.rearrange("(c p) o -> p (c o)", p=P))
 
         ident = keep.tile([P, P], F32, name="ident")
         make_identity(nc, ident[:])
-
-        warm = keep.tile([P, 1], F32, name="warm")
-        nc.scalar.activation(out=warm[:], in_=ident[:, 0:1], func=ACT.Exp)
 
         neg_dsc = keep.tile([P, PACK], F32, name="neg_dsc")
         nc.scalar.activation(out=neg_dsc[:], in_=dsc_t[:], func=ACT.Copy, scale=-1.0)
@@ -72,28 +70,36 @@ def tile_attend_similarmerge_pl_kernel(tc, query, keys, steep, th, dsc, offs, of
         move_banks = [psum.tile([P, PACK * P], F32, name="move%d" % c) for c in range(CHUNKS)]
         spread_bank = move_banks[0]
 
-        def scale_rows(on_vector, out, in_, factor):
+        slot_columns = move_banks[1][:, 0:P]
+        nc.tensor.transpose(slot_columns, slot_rows[:], ident[:])
+        term_bias = keep.tile([P, CHUNKS], F32, name="term_bias")
+        tanh_scale = keep.tile([P, CHUNKS], F32, name="tanh_scale")
+        nc.scalar.activation(out=term_bias[:], in_=slot_columns[:, 0:CHUNKS], func=ACT.Copy, scale=-float(D // P))
+        nc.scalar.activation(out=tanh_scale[:], in_=slot_columns[:, CHUNKS:2 * CHUNKS], func=ACT.Copy, scale=0.5 / D)
+
+        def times_factor(on_vector, out, in_, factor):
             if on_vector:
                 nc.vector.tensor_scalar(out, in_, factor, None, ALU.mult)
             else:
                 nc.scalar.activation(out=out, in_=in_, func=ACT.Copy, scale=factor)
 
-        def gather(t, first, count, two_input, scale_on_vector=False):
+        def gather(t, first, count, product_on, difference_on, scale_on_vector=False):
             cols = slice(first // PER_COLUMN, (first + count) // PER_COLUMN)
             piece = "%d_%d" % (t, first)
             pair = keep.tile([P, 2 * count], F32, name="pair" + piece, tag="pair" + piece, align_bytes=64)
             ka, kb = pair[:, 0:count], pair[:, count:2 * count]
             nc.vector.tensor_copy(ka, planes[t][:].indirect(offs_a[:, cols]))
             nc.vector.tensor_copy(kb, planes[t][:].indirect(offs_b[:, cols]))
-            scale_rows(scale_on_vector, neg_ka[:, t, first:first + count], ka, neg_dsc[:, t:t + 1])
+            times_factor(scale_on_vector, neg_ka[:, t, first:first + count], ka, neg_dsc[:, t:t + 1])
             prod = keep.tile([P, count], F32, name="prod" + piece)
-            two_input.tensor_tensor(prod[:], ka, kb, ALU.mult)
+            product_on.tensor_tensor(prod[:], ka, kb, ALU.mult)
             spread = min(max(HALF - first, 0), count)
             if spread < count:
                 kb_s = keep.tile([P, count], F32, name="kb_s" + piece)
-                scale_rows(scale_on_vector, kb_s[:, spread:count], kb[:, spread:count], dsc_t[:, t:t + 1])
+                times_factor(scale_on_vector, kb_s[:, spread:count], kb[:, spread:count], dsc_t[:, t:t + 1])
             if spread > 0:
-                two_input.tensor_tensor(diff[:, t, first:first + spread], kb[:, 0:spread], ka[:, 0:spread], ALU.subtract)
+                difference_on.tensor_tensor(diff[:, t, first:first + spread], kb[:, 0:spread], ka[:, 0:spread],
+                                            ALU.subtract)
             for c in range(first // CHUNK, (first + count) // CHUNK):
                 here = slice(c * CHUNK - first, (c + 1) * CHUNK - first)
                 nc.tensor.matmul(dot_banks[c][:, 0:P], prod[:, here], ident[:], is_transpose=True,
@@ -114,18 +120,13 @@ def tile_attend_similarmerge_pl_kernel(tc, query, keys, steep, th, dsc, offs, of
                     in_=q_raw[h][:, :, PACK * s0:PACK * (s0 + ROUND_STEP)].rearrange("p t (s r) -> p s t r", r=PACK),
                 )
 
-        gather(0, 0, I, nc.gpsimd)
+        gather(0, 0, I, nc.gpsimd, nc.gpsimd)
         round_query(0)
-        gather(1, 0, I, nc.gpsimd)
+        gather(1, 0, I, nc.gpsimd, nc.gpsimd)
         round_query(1)
-        gather(2, 0, HALF, nc.gpsimd)
-        gather(2, HALF, HALF, nc.vector)
-        tanh_scale = keep.tile([P, CHUNKS], F32, name="tanh_scale")
-        term_bias = keep.tile([P, CHUNKS], F32, name="term_bias")
-        nc.scalar.activation(out=tanh_scale[:], in_=steep_t[:], func=ACT.Copy, scale=0.5 / D)
-        nc.scalar.activation(out=term_bias[:], in_=th_t[:], func=ACT.Copy, scale=-float(D // P))
+        gather(2, 0, I, nc.vector, nc.gpsimd)
         for c in range(CHUNKS):
-            gather(PACK - 1, c * CHUNK, CHUNK, nc.vector, scale_on_vector=c * CHUNK >= HALF)
+            gather(PACK - 1, c * CHUNK, CHUNK, nc.vector, nc.vector, scale_on_vector=c * CHUNK >= HALF)
 
         q_codes = keep.tile([P, Q], U32, name="q_codes", align_bytes=64)
         q_scales = keep.tile([P, Q], U8, name="q_scales", tag="pair%d_%d" % (PACK - 1, CHUNK), align_bytes=64)
@@ -137,7 +138,8 @@ def tile_attend_similarmerge_pl_kernel(tc, query, keys, steep, th, dsc, offs, of
         def weigh(c):
             col = slice(c, c + 1)
             turned = c * CHUNK >= HALF
-            terms = keep.tile([P, P], F32, name="terms%d" % c, tag="tanh%d" % (c - 1) if turned else "terms%d" % c)
+            first_turned = c * CHUNK == HALF
+            terms = keep.tile([P, P], F32, name="terms%d" % c, tag="tanh%d" % (c - 1) if first_turned else "terms%d" % c)
             nc.scalar.activation(out=terms[:], in_=dot_banks[c][:, 0:P], func=ACT.Identity, bias=term_bias[:, col],
                                  accum_out=centred[:, col])
             tanh_c = keep.tile([P, 1], F32, name="tanh%d" % c, tag="tanh%d" % c)
@@ -202,34 +204,28 @@ def tile_attend_similarmerge_pl_kernel(tc, query, keys, steep, th, dsc, offs, of
         y_bf = keep.tile([P, I, PACK], BF16, name="y_bf", align_bytes=64)
         out_v = out_0.rearrange("(p r) n -> p r n", r=PACK)
 
-        def round_pair(pair, cols):
-            two = slice(2 * pair, 2 * pair + 2)
-            nc.vector.tensor_copy(
-                y_bf[:, cols, two].rearrange("p (a i) r -> p a r i", i=RUN),
-                y[:, two, cols].rearrange("p r (a i) -> p a r i", i=RUN),
-            )
-
         for r in range(PACK):
             nc.vector.tensor_reduce(neg_max[:, r:r + 1], score_banks[r][:], AXIS_X, ALU.max, negate=True)
             nc.scalar.activation(out=probs[:, r, :], in_=score_banks[r][:], func=ACT.Exp, bias=neg_max[:, r:r + 1],
                                  accum_out=sums[:, r:r + 1])
         for r in range(PACK):
             nc.vector.reciprocal(inverse[:, r:r + 1], sums[:, r:r + 1])
-            nc.vector.tensor_scalar(y[:, r, :], probs[:, r, :], inverse[:, r:r + 1], float(I), ALU.mult, ALU.mult)
+            nc.vector.tensor_scalar(y[:, r, :], probs[:, r, :], inverse[:, r:r + 1], OUT_SCALE, ALU.mult, ALU.mult)
             nc.sync.dma_start(out=out_v[:, r, :], in_=y[:, r, :])
-            if r == 1:
-                round_pair(0, slice(0, I))
 
         y_codes = keep.tile([P, I], U32, name="y_codes", align_bytes=64)
         y_scales = keep.tile([P, I], U8, name="y_scales", align_bytes=64)
         words = out_1.rearrange("z p c r -> p (z c r)").bitcast(I32)
         for h, queue in enumerate((nc.sync, nc.scalar)):
             cols = slice(h * HALF, (h + 1) * HALF)
-            round_pair(1, cols)
+            nc.vector.tensor_copy(
+                y_bf[:, cols, :].rearrange("p (a i) r -> p a r i", i=RUN),
+                y[:, :, cols].rearrange("p r (a i) -> p a r i", i=RUN),
+            )
             nc.vector.quantize_mx(out=y_codes[:, cols].bitcast(FP8X4), scales=y_scales[:, cols],
                                   in_=y_bf[:, cols, :].rearrange("p n r -> p (n r)"))
             queue.dma_start(out=words[:, cols], in_=y_codes[:, cols].bitcast(I32))
-        scale_rows_out = out_2.rearrange("z q c -> (z q) c").bitcast(I32)
+        scale_bytes = out_2.rearrange("z q c -> (z q) c").bitcast(I32)
         for j, queue in enumerate((nc.sync, nc.sync, nc.sync, nc.scalar)):
-            queue.dma_start(out=scale_rows_out[PACK * j:PACK * (j + 1), :],
-                            in_=y_scales[QUADRANT * j:QUADRANT * j + PACK, :].bitcast(I32))
+            queue.dma_start(out=scale_bytes[SCALE_ROWS * j:SCALE_ROWS * (j + 1), :],
+                            in_=y_scales[QUADRANT * j:QUADRANT * j + SCALE_ROWS, :].bitcast(I32))

from contextlib import ExitStack

import concourse.mybir as mybir
from concourse.masks import make_identity

F32 = mybir.dt.float32
BF16 = mybir.dt.bfloat16
U32 = mybir.dt.uint32
I32 = mybir.dt.int32
U16 = mybir.dt.uint16
U8 = mybir.dt.uint8
FP8X4 = mybir.dt.float8_e4m3fn_x4
ALU = mybir.AluOpType
ACT = mybir.ActivationFunctionType
AXIS_X = mybir.AxisListType.X

P = 128
PACK = 4
D, T, I, Q = 512, 1024, 512, 512
CHUNK = 128
CHUNKS = I // CHUNK
HALF = I // 2
PER_COLUMN = 16
RUN = 4
ROUND_STEP = 32
QUADRANT = 32
SCALE_ROWS = 4
OUT_SCALE = 512.0

FLOPS = 2 * D * I * Q


def tile_attend_similarmerge_pl_kernel(tc, query, keys, steep, th, dsc, offs, offs2, out_0, out_1, out_2):
    nc = tc.nc
    with ExitStack() as ctx:
        keep = ctx.enter_context(tc.tile_pool(name="keep", bufs=1))
        psum = ctx.enter_context(tc.psum_pool(name="psum", bufs=1))

        offs_a = keep.tile([P, I // PER_COLUMN], U16, name="offs_a")
        offs_b = keep.tile([P, I // PER_COLUMN], U16, name="offs_b")
        planes = [keep.tile([P, T], F32, name="plane%d" % t) for t in range(PACK)]
        q_raw = [keep.tile([P, PACK, Q // 2], F32, name="q_raw%d" % h) for h in range(2)]
        dsc_t = keep.tile([P, PACK], F32, name="dsc_t")
        slot_rows = keep.tile([P, P], F32, name="slot_rows")
        nc.gpsimd.memset(slot_rows[:], 0.0)
        nc.scalar.dma_start(out=slot_rows[0:CHUNKS, :], in_=th.rearrange("(c p) o -> c (p o)", p=P))
        nc.scalar.dma_start(out=slot_rows[CHUNKS:2 * CHUNKS, :], in_=steep.rearrange("(c p) o -> c (p o)", p=P))

        keys_v = keys.rearrange("(p t) n -> p t n", t=PACK)
        query_v = query.rearrange("(p t) n -> p t n", t=PACK)
        nc.sync.dma_start(out=planes[0][:], in_=keys_v[:, 0, :])
        nc.sync.dma_start(offs_a[:], offs)
        nc.sync.dma_start(offs_b[:], offs2)
        nc.sync.dma_start(out=dsc_t[:], in_=dsc.rearrange("o (p t) -> p (o t)", t=PACK))
        nc.sync.dma_start(out=q_raw[0][:], in_=query_v[:, :, 0:Q // 2])
        nc.sync.dma_start(out=planes[1][:], in_=keys_v[:, 1, :])
        nc.sync.dma_start(out=q_raw[1][:], in_=query_v[:, :, Q // 2:Q])
        nc.sync.dma_start(out=planes[2][:], in_=keys_v[:, 2, :])
        nc.sync.dma_start(out=planes[3][:], in_=keys_v[:, 3, :])

        ident = keep.tile([P, P], F32, name="ident")
        make_identity(nc, ident[:])

        neg_dsc = keep.tile([P, PACK], F32, name="neg_dsc")
        nc.scalar.activation(out=neg_dsc[:], in_=dsc_t[:], func=ACT.Copy, scale=-1.0)

        neg_ka = keep.tile([P, PACK, I], F32, name="neg_ka")
        diff = keep.tile([P, PACK, HALF], F32, name="diff")
        dot_banks = [psum.tile([P, PACK * P], F32, name="dot%d" % c) for c in range(CHUNKS)]
        move_banks = [psum.tile([P, PACK * P], F32, name="move%d" % c) for c in range(CHUNKS)]
        spread_bank = move_banks[0]

        slot_columns = move_banks[1][:, 0:P]
        nc.tensor.transpose(slot_columns, slot_rows[:], ident[:])
        term_bias = keep.tile([P, CHUNKS], F32, name="term_bias")
        tanh_scale = keep.tile([P, CHUNKS], F32, name="tanh_scale")
        nc.scalar.activation(out=term_bias[:], in_=slot_columns[:, 0:CHUNKS], func=ACT.Copy, scale=-float(D // P))
        nc.scalar.activation(out=tanh_scale[:], in_=slot_columns[:, CHUNKS:2 * CHUNKS], func=ACT.Copy, scale=0.5 / D)

        def times_factor(on_vector, out, in_, factor):
            if on_vector:
                nc.vector.tensor_scalar(out, in_, factor, None, ALU.mult)
            else:
                nc.scalar.activation(out=out, in_=in_, func=ACT.Copy, scale=factor)

        def gather(t, first, count, product_on, difference_on, scale_on_vector=False):
            cols = slice(first // PER_COLUMN, (first + count) // PER_COLUMN)
            piece = "%d_%d" % (t, first)
            pair = keep.tile([P, 2 * count], F32, name="pair" + piece, tag="pair" + piece, align_bytes=64)
            ka, kb = pair[:, 0:count], pair[:, count:2 * count]
            nc.vector.tensor_copy(ka, planes[t][:].indirect(offs_a[:, cols]))
            nc.vector.tensor_copy(kb, planes[t][:].indirect(offs_b[:, cols]))
            times_factor(scale_on_vector, neg_ka[:, t, first:first + count], ka, neg_dsc[:, t:t + 1])
            prod = keep.tile([P, count], F32, name="prod" + piece)
            product_on.tensor_tensor(prod[:], ka, kb, ALU.mult)
            spread = min(max(HALF - first, 0), count)
            if spread < count:
                kb_s = keep.tile([P, count], F32, name="kb_s" + piece)
                times_factor(scale_on_vector, kb_s[:, spread:count], kb[:, spread:count], dsc_t[:, t:t + 1])
            if spread > 0:
                difference_on.tensor_tensor(diff[:, t, first:first + spread], kb[:, 0:spread], ka[:, 0:spread],
                                            ALU.subtract)
            for c in range(first // CHUNK, (first + count) // CHUNK):
                here = slice(c * CHUNK - first, (c + 1) * CHUNK - first)
                nc.tensor.matmul(dot_banks[c][:, 0:P], prod[:, here], ident[:], is_transpose=True,
                                 start=t == 0, stop=t == PACK - 1)
                if c * CHUNK >= HALF:
                    target = move_banks[c][:, t * P:(t + 1) * P]
                    nc.tensor.matmul(target, neg_ka[:, t, c * CHUNK:(c + 1) * CHUNK], ident[:], is_transpose=True,
                                     start=True, stop=False)
                    nc.tensor.matmul(target, kb_s[:, here], ident[:], is_transpose=True, start=False, stop=True)

        q_bf = keep.tile([P, PACK, P, PACK], BF16, name="q_bf", align_bytes=64)

        def round_query(h):
            for s0 in range(0, P // 2, ROUND_STEP):
                place = h * P // 2 + s0
                nc.scalar.copy(
                    out=q_bf[:, :, place:place + ROUND_STEP, :].rearrange("p r s t -> p s t r"),
                    in_=q_raw[h][:, :, PACK * s0:PACK * (s0 + ROUND_STEP)].rearrange("p t (s r) -> p s t r", r=PACK),
                )

        gather(0, 0, I, nc.gpsimd, nc.gpsimd)
        round_query(0)
        gather(1, 0, I, nc.gpsimd, nc.gpsimd)
        round_query(1)
        gather(2, 0, I, nc.vector, nc.gpsimd)
        for c in range(CHUNKS):
            gather(PACK - 1, c * CHUNK, CHUNK, nc.vector, nc.vector, scale_on_vector=c * CHUNK >= HALF)

        q_codes = keep.tile([P, Q], U32, name="q_codes", align_bytes=64)
        q_scales = keep.tile([P, Q], U8, name="q_scales", tag="pair%d_%d" % (PACK - 1, CHUNK), align_bytes=64)
        nc.vector.quantize_mx(out=q_codes[:].bitcast(FP8X4), scales=q_scales[:],
                              in_=q_bf[:].rearrange("p r s t -> p (r s t)"))

        centred = keep.tile([P, CHUNKS], F32, name="centred")

        def weigh(c):
            col = slice(c, c + 1)
            turned = c * CHUNK >= HALF
            first_turned = c * CHUNK == HALF
            terms = keep.tile([P, P], F32, name="terms%d" % c, tag="tanh%d" % (c - 1) if first_turned else "terms%d" % c)
            nc.scalar.activation(out=terms[:], in_=dot_banks[c][:, 0:P], func=ACT.Identity, bias=term_bias[:, col],
                                 accum_out=centred[:, col])
            tanh_c = keep.tile([P, 1], F32, name="tanh%d" % c, tag="tanh%d" % c)
            nc.scalar.activation(out=tanh_c[:], in_=centred[:, col], func=ACT.Tanh, scale=tanh_scale[:, col])
            if turned:
                share = keep.tile([P, 1], F32, name="share%d" % c)
                nc.scalar.activation(out=share[:], in_=tanh_c[:], func=ACT.Copy, scale=0.25, bias=0.25)
                step = keep.tile([P, PACK * P], F32, name="step%d" % c)
                nc.scalar.activation(out=step[:], in_=move_banks[c][:], func=ACT.Copy, scale=share[:])
                for t in range(PACK):
                    nc.tensor.transpose(dot_banks[c][:, t * P:(t + 1) * P], step[:, t * P:(t + 1) * P], ident[:])
            else:
                share = keep.tile([P, P], F32, name="share%d" % c)
                nc.scalar.activation(out=share[:], in_=tanh_c[:].to_broadcast([P, P]), func=ACT.Copy, scale=0.25, bias=0.25)
                nc.tensor.transpose(spread_bank[:, c * CHUNK:(c + 1) * CHUNK], share[:], ident[:])

        k_codes = keep.tile([P, I], U32, name="k_codes", align_bytes=64)
        k_scales = keep.tile([P, I], U8, name="k_scales", align_bytes=64)

        def merge(c):
            slots = slice(c * CHUNK, (c + 1) * CHUNK)
            if c * CHUNK >= HALF:
                moved = dot_banks[c][:].rearrange("p (t n) -> p t n", t=PACK)
            else:
                moved = spread_moved[:, :, slots]
            km = keep.tile([P, CHUNK, PACK], BF16, name="km%d" % c, align_bytes=64)
            nc.vector.tensor_tensor(
                km[:].rearrange("p (a i) t -> p a t i", i=RUN),
                moved.rearrange("p t (a i) -> p a t i", i=RUN),
                neg_ka[:, :, slots].rearrange("p t (a i) -> p a t i", i=RUN),
                ALU.subtract,
            )
            nc.vector.quantize_mx(out=k_codes[:, slots].bitcast(FP8X4), scales=k_scales[:, slots],
                                  in_=km[:].rearrange("p n t -> p (n t)"))

        for c in range(CHUNKS):
            weigh(c)
        spread_moved = keep.tile([P, PACK, HALF], F32, name="spread_moved")
        for t in range(PACK):
            nc.vector.scalar_tensor_tensor(spread_moved[:, t, :], diff[:, t, :], dsc_t[:, t:t + 1],
                                           spread_bank[:, 0:HALF], ALU.mult, ALU.mult)
        for c in range(CHUNKS):
            merge(c)

        score_banks = [move_banks[1], dot_banks[0], dot_banks[1], move_banks[0]]
        for first in range(0, I, HALF):
            slots = slice(first, first + HALF)
            for r in range(PACK):
                rows = slice(r * P, (r + 1) * P)
                nc.tensor.matmul_mx(
                    out=score_banks[r][:, slots],
                    lhsT=q_codes[:, rows].bitcast(FP8X4), lhsT_scale=q_scales[:, rows],
                    rhs=k_codes[:, slots].bitcast(FP8X4), rhs_scale=k_scales[:, slots],
                    start=True, stop=True,
                )

        neg_max = keep.tile([P, PACK], F32, name="neg_max")
        sums = keep.tile([P, PACK], F32, name="sums")
        inverse = keep.tile([P, PACK], F32, name="inverse")
        probs = keep.tile([P, PACK, I], F32, name="probs")
        y = keep.tile([P, PACK, I], F32, name="y")
        y_bf = keep.tile([P, I, PACK], BF16, name="y_bf", align_bytes=64)
        out_v = out_0.rearrange("(p r) n -> p r n", r=PACK)

        for r in range(PACK):
            nc.vector.tensor_reduce(neg_max[:, r:r + 1], score_banks[r][:], AXIS_X, ALU.max, negate=True)
            nc.scalar.activation(out=probs[:, r, :], in_=score_banks[r][:], func=ACT.Exp, bias=neg_max[:, r:r + 1],
                                 accum_out=sums[:, r:r + 1])
        for r in range(PACK):
            nc.vector.reciprocal(inverse[:, r:r + 1], sums[:, r:r + 1])
            nc.vector.tensor_scalar(y[:, r, :], probs[:, r, :], inverse[:, r:r + 1], OUT_SCALE, ALU.mult, ALU.mult)
            nc.sync.dma_start(out=out_v[:, r, :], in_=y[:, r, :])

        y_codes = keep.tile([P, I], U32, name="y_codes", align_bytes=64)
        y_scales = keep.tile([P, I], U8, name="y_scales", align_bytes=64)
        words = out_1.rearrange("z p c r -> p (z c r)").bitcast(I32)
        for h, queue in enumerate((nc.sync, nc.scalar)):
            cols = slice(h * HALF, (h + 1) * HALF)
            nc.vector.tensor_copy(
                y_bf[:, cols, :].rearrange("p (a i) r -> p a r i", i=RUN),
                y[:, :, cols].rearrange("p r (a i) -> p a r i", i=RUN),
            )
            nc.vector.quantize_mx(out=y_codes[:, cols].bitcast(FP8X4), scales=y_scales[:, cols],
                                  in_=y_bf[:, cols, :].rearrange("p n r -> p (n r)"))
            queue.dma_start(out=words[:, cols], in_=y_codes[:, cols].bitcast(I32))
        scale_bytes = out_2.rearrange("z q c -> (z q) c").bitcast(I32)
        for j, queue in enumerate((nc.sync, nc.sync, nc.sync, nc.scalar)):
            queue.dma_start(out=scale_bytes[SCALE_ROWS * j:SCALE_ROWS * (j + 1), :],
                            in_=y_scales[QUADRANT * j:QUADRANT * j + SCALE_ROWS, :].bitcast(I32))
